import numpy as np
import ml_dtypes


def mxq(x, axis, fmt="e4m3"):
    dtype, down = {"e4m3": (ml_dtypes.float8_e4m3fn, 7), "e5m2": (ml_dtypes.float8_e5m2, 14)}[fmt]
    v = np.moveaxis(np.asarray(x, np.float32).astype(ml_dtypes.bfloat16).astype(np.float64), axis, -1)
    blocks = v.reshape(v.shape[:-1] + (-1, 32))
    amax = np.abs(blocks).max(-1, keepdims=True)
    byte = np.maximum(np.where(amax > 0, np.frexp(amax)[1] - 1 + 127, 0) - down, 1)
    scale = np.exp2(byte - 127.0)
    codes = (blocks / scale).astype(np.float32).astype(dtype).astype(np.float64)
    return np.moveaxis((codes * scale).reshape(v.shape), -1, axis)


WIDE = False


def mx_kscale(k):
    if not WIDE:
        return np.ones(k)
    levels = np.array([10, -10, 5, -5, 0])
    if k % 512:
        return np.exp2(np.random.permutation(np.resize(levels, k // 32))).repeat(32)
    a = np.empty((k // 512, 16))
    for p in range(k // 512):
        a[p, :8] = np.random.permutation(np.resize(levels, 8))
        for g in range(8):
            far = levels[np.abs(levels - a[p, g]) >= 10]
            a[p, g + 8] = far[np.random.randint(len(far))]
    return np.exp2(a.ravel()).repeat(32)


BF16 = ml_dtypes.bfloat16


def bf(x):
    return np.asarray(x, np.float32).astype(BF16)


def f64(x):
    return np.asarray(x).astype(np.float64)


E2M1 = np.array([0.0, 0.5, 1.0, 1.5, 2.0, 3.0, 4.0, 6.0, -0.0, -0.5, -1.0, -1.5, -2.0, -3.0, -4.0, -6.0])


def pack_weight(w, fmt):
    k, n = w.shape
    w = f64(bf(w)).reshape(k // 32, 32, n)
    amax = np.abs(w).max(1)
    if fmt == "e4m3":
        byte = np.frexp(amax)[1] - 1 + 127 - 7
    else:
        mant, ex = np.frexp(amax / 6.0)
        byte = np.where(mant > 0.5, ex, ex - 1) + 127
    byte = np.clip(np.where(amax > 0, byte, 1), 1, 254)
    scaled = (w * np.exp2(127.0 - byte)[:, None, :]).reshape(k, n).astype(np.float32)
    by_word = np.ascontiguousarray(scaled.reshape(k // 512, 128, 4, n).transpose(0, 1, 3, 2))
    if fmt == "e4m3":
        words = by_word.astype(ml_dtypes.float8_e4m3fn).view(np.uint8)
    else:
        c = by_word.astype(ml_dtypes.float4_e2m1fn).view(np.uint8) & 0xF
        words = c[..., 0::2] | (c[..., 1::2] << 4)
    return np.ascontiguousarray(words), np.ascontiguousarray(byte.astype(np.uint8).reshape(k // 512, 16, n))


def unpack_weight(words, scales, fmt):
    g, p, n, _ = words.shape
    if fmt == "e4m3":
        vals = np.ascontiguousarray(words).view(ml_dtypes.float8_e4m3fn).astype(np.float64)
    else:
        nib = np.empty((g, p, n, 4), np.uint8)
        nib[..., 0::2] = words & 0xF
        nib[..., 1::2] = words >> 4
        vals = E2M1[nib]
    vals = vals * np.repeat(np.exp2(scales.astype(np.float64) - 127.0), 8, axis=1)[..., None]
    return vals.transpose(0, 1, 3, 2).reshape(g * 512, n)
def pack4(w):
    words, scales = pack_weight(w, "e2m1")
    return words.reshape(words.shape[0], 128, -1), scales


def unpack4(words, scales):
    return unpack_weight(words.reshape(words.shape[0], 128, -1, 2), scales, "e2m1")


E4M3FN = np.array([(-1.0 if i & 128 else 1.0) * ((1.0 + (i & 7) / 8.0) * 2.0 ** (((i >> 3) & 15) - 7) if i & 120 else (i & 7) * 2.0 ** -9) for i in range(256)])


def e4m3fn_bytes(y):
    return np.clip(np.asarray(y, np.float64), -448.0, 448.0).astype(np.float32).astype(ml_dtypes.float8_e4m3fn).view(np.uint8)


def e4m3fn_values(b):
    return E4M3FN[b]


T, R, K, F, N, B = 2048, 4, 1024, 1024, 1024, 128
FP8_MAX = 448.0
GELU_A, GELU_B = np.sqrt(2.0 / np.pi), 0.044715


def setup_inputs():
    s = mx_kscale(K)
    t = mx_kscale(R * F)
    x = np.random.standard_normal((T, K)) * s
    x_scale = (np.abs(x).reshape(T, K // B, B).max(axis=2) / FP8_MAX).astype(np.float32)
    x_bytes = e4m3fn_bytes(x / np.repeat(f64(x_scale), B, axis=1))
    w2 = np.random.standard_normal((R * F, N)) / np.sqrt(R * F) / t[:, None]
    w2_words, w2_scales = pack4(w2)
    return {"x_bytes": x_bytes,
            "x_scale": x_scale,
            "w1": bf(np.random.standard_normal((K, F)) / np.sqrt(K) / s[:, None]),
            "gain": bf((1 + 0.1 * np.random.standard_normal(R * F)) * t),
            "w2_words": w2_words,
            "w2_scales": w2_scales,
            "b": bf(0.3 * np.random.standard_normal(N))}


def reference(x_bytes, x_scale, w1, gain, w2_words, w2_scales, b):
    x = e4m3fn_values(x_bytes) * np.repeat(f64(x_scale), B, axis=1)
    h = mxq(x, 1, "e4m3") @ mxq(f64(w1), 0, "e4m3")
    a = 0.5 * h * (1.0 + np.tanh(GELU_A * (h + GELU_B * h * h * h)))
    z = a.reshape(T // R, R * F) * f64(gain)
    y = (mxq(z, 1, "e4m3") @ unpack4(w2_words, w2_scales)) + f64(b)
    return y

@@ -1,0 +1,501 @@
+from contextlib import ExitStack
+
+import concourse.mybir as mybir
+from concourse.masks import make_identity
+
+T, R, K, F, N = 2048, 4, 1024, 1024, 1024
+FLOPS = 2 * T * K * F + 2 * (T // R) * (R * F) * N
+
+F32 = mybir.dt.float32
+BF16 = mybir.dt.bfloat16
+I32 = mybir.dt.int32
+U32 = mybir.dt.uint32
+U8 = mybir.dt.uint8
+FP8 = mybir.dt.float8_e4m3fn
+FP8X4 = mybir.dt.float8_e4m3fn_x4
+FP4X4 = mybir.dt.float4_e2m1fn_x4
+MULT = mybir.AluOpType.mult
+ADD = mybir.AluOpType.add
+COPY = mybir.ActivationFunctionType.Copy
+GELU = mybir.ActivationFunctionType.Gelu_apprx_tanh
+
+P = 128
+GROUPS = 4
+PAIRS = 8
+XW_BUFS = 10
+UNITS = [(0, 0), (1, 0), (0, 1), (1, 1)] + [(pair, g) for pair in range(2, PAIRS) for g in range(2)]
+
+
+def tile_image_token_merger_d4_kernel(tc, x_bytes, x_scale, w1, gain, w2_words, w2_scales, b, out):
+    nc = tc.nc
+    with ExitStack() as ctx:
+        keep = ctx.enter_context(tc.tile_pool(name="keep", bufs=1))
+        work = ctx.enter_context(tc.tile_pool(name="work", bufs=4))
+        psum = ctx.enter_context(tc.psum_pool(name="psum", bufs=1))
+        ctx.enter_context(tc.manual_schedule())
+
+        ident = keep.tile([P, P], F32, name="ident")
+        make_identity(nc, ident[:])
+        warm = keep.tile([P, 8], F32, name="warm")
+        nc.vector.memset(warm[:, 0:1], 0.0)
+        nc.scalar.activation(out=warm[:, 4:5], in_=warm[:, 0:1], func=GELU)
+
+        gain_rows = keep.tile([P, 512], BF16, name="gain_rows")
+        nc.vector.memset(gain_rows[:].bitcast(I32), 0)
+        w2s = [keep.tile([P, R, N], U8, name="w2s%d" % g, align_bytes=64) for g in range(2)]
+        for g in range(2):
+            nc.vector.memset(w2s[g][:].rearrange("p j n -> p (j n)").bitcast(I32), 0)
+
+        xs = keep.tile([P, GROUPS, 32], F32, name="xs")
+        xb = [keep.tile([P, 2 * K], U8, name="xb%d" % i) for i in range(PAIRS)]
+        w1raw = [[keep.tile([P, 4, 512], BF16, name="w1raw%d%d" % (c, g)) for g in range(2)] for c in range(2)]
+        w2w = [keep.tile([P, 2 * N], U8, name="w2w%d" % i, align_bytes=64) for i in range(8)]
+        bias = keep.tile([P, N], BF16, name="bias")
+        x_rows = x_bytes.rearrange("(G m i jj) k -> G i m (jj k)", m=P, i=2, jj=2)
+        w1_rows = w1.rearrange("(c p s) f -> c p s f", p=P, s=4)
+        w2s_rows = w2_scales.rearrange("(j g) r n -> g r j n", g=2)
+
+        def load_x(pair, lo=0, hi=2):
+            cols = slice(K * lo, K * hi)
+            nc.sync.dma_start(out=xb[pair][:, cols], in_=x_rows[pair // 2, pair % 2][:, cols])
+
+        def load_w1(c, g):
+            nc.sync.dma_start(out=w1raw[c][g][:], in_=w1_rows[c, :, :, 512 * g : 512 * (g + 1)])
+
+        def load_w2_scales(g, q):
+            nc.sync.dma_start(
+                out=w2s[g][32 * q : 32 * q + 4, :, :].bitcast(I32),
+                in_=w2s_rows[g, 4 * q : 4 * q + 4].bitcast(I32),
+            )
+
+        def load_w2(i):
+            nc.sync.dma_start(out=w2w[i][:].bitcast(I32), in_=w2_words[i].bitcast(I32))
+
+        modes = {}
+        xw, xt, xg, xq, w1g, w1q, hb, act, zg, zq, yb = {}, {}, {}, {}, {}, {}, {}, {}, {}, {}, {}
+
+        def widen(pair, jj, c, mode):
+            xw[pair, jj, c] = work.tile([P, 512], BF16, name="xw", bufs=XW_BUFS)
+            modes[pair, jj, c] = mode
+            dst = xw[pair, jj, c]
+            if mode == "D":
+                dst = work.tile([P, 512], BF16, name="xnat", bufs=2)
+            for q in range(4):
+                blk = 4 * c + q
+                col = 8 * (2 * (pair % 2) + jj) + blk
+                src = xb[pair][:, K * jj + 128 * blk : K * jj + 128 * (blk + 1)].bitcast(FP8)
+                scale = xs[:, pair // 2, col : col + 1]
+                if mode == "V":
+                    nc.vector.tensor_scalar(
+                        out=dst[:].rearrange("m (u p e) -> m p u e", u=2, e=2)[:, 32 * q : 32 * (q + 1), :, :],
+                        in0=src.rearrange("m (p u e) -> m p u e", u=2, e=2),
+                        scalar1=scale,
+                        scalar2=None,
+                        op0=MULT,
+                    )
+                else:
+                    nc.scalar.activation(out=dst[:, 128 * q : 128 * (q + 1)], in_=src, func=COPY, scale=scale)
+            if mode == "D":
+                nc.scalar.copy(
+                    out=xw[pair, jj, c][:].bitcast(F32).rearrange("m (u p) -> m u p", u=2),
+                    in_=dst[:].bitcast(F32).rearrange("m (p u) -> m u p", u=2),
+                )
+
+        def turn(pair, jj):
+            xt[pair, jj] = psum.tile([P, 2, 2, P], F32, name="xt", bufs=2)
+            for c in range(2):
+                words = xw[pair, jj, c][:].bitcast(F32)
+                for u in range(2):
+                    src = words[:, u : 256 : 2] if modes[pair, jj, c] == "S" else words[:, P * u : P * (u + 1)]
+                    nc.tensor.transpose(xt[pair, jj][:, c, u, :], src, ident[:])
+
+        def gather(pair, jj):
+            if pair not in xg:
+                xg[pair] = work.tile([P, 2, 2, P, 2], F32, name="xg", bufs=3, align_bytes=64)
+            nc.scalar.copy(out=xg[pair][:, :, jj, :, :], in_=xt[pair, jj][:].rearrange("p c u m -> p c m u"))
+
+        def quant_x(pair):
+            codes = work.tile([P, 512], U32, name="xcodes", bufs=4, align_bytes=64)
+            scales = work.tile([P, 512], U8, name="xscales", bufs=4, align_bytes=64)
+            src = xg[pair][:].rearrange("p c jj m u -> p (c jj m u)").bitcast(BF16)
+            nc.vector.quantize_mx(out=codes[:].bitcast(FP8X4), scales=scales[:], in_=src)
+            xq[pair] = (codes, scales)
+
+        def group_w1(c, g, u, mode):
+            w1g[c, g, u] = keep.tile([P, 2, P, 4], BF16, name="w1g%d%d%d" % (c, g, u), align_bytes=64)
+            copy = nc.vector.tensor_copy if mode == "V" else nc.scalar.copy
+            copy(
+                out=w1g[c, g, u][:].rearrange("p t m s -> p m s t"),
+                in_=w1raw[c][g][:].rearrange("p s (m t) -> p m s t", t=4)[:, :, :, 2 * u : 2 * u + 2],
+            )
+
+        def quant_w1(c, g, u):
+            codes = keep.tile([P, 256], U32, name="w1codes%d%d%d" % (c, g, u), align_bytes=64)
+            scales = keep.tile([P, 256], U8, name="w1scales%d%d%d" % (c, g, u), align_bytes=64)
+            src = w1g[c, g, u][:].rearrange("p t m s -> p (t m s)")
+            nc.vector.quantize_mx(out=codes[:].bitcast(FP8X4), scales=scales[:], in_=src)
+            w1q[c, g, u] = (codes, scales)
+
+        def first_product(s, u):
+            pair, g = UNITS[s]
+            hb[s, u] = psum.tile([P, 2, 256], F32, name="hb", bufs=3)
+            for e in range(2):
+                cols = slice(P * e, P * (e + 1))
+                for c in range(2):
+                    toks = slice(256 * c, 256 * (c + 1))
+                    nc.tensor.matmul_mx(
+                        out=hb[s, u][:, e, :],
+                        lhsT=w1q[c, g, u][0][:, cols].bitcast(FP8X4),
+                        lhsT_scale=w1q[c, g, u][1][:, cols],
+                        rhs=xq[pair][0][:, toks].bitcast(FP8X4),
+                        rhs_scale=xq[pair][1][:, toks],
+                        start=(c == 0),
+                        stop=(c == 1),
+                    )
+
+        def gelu(s, u):
+            if s not in act:
+                act[s] = work.tile([P, 2, 256, 2], F32, name="act", bufs=6)
+            nc.scalar.activation(out=act[s][:, u, :, :], in_=hb[s, u][:].rearrange("p e n -> p n e"), func=GELU)
+
+        def apply_gain(s, jj):
+            pair, g = UNITS[s]
+            if s not in zg:
+                zg[s] = work.tile([P, 2, P, 2, 2], BF16, name="zg", bufs=3, align_bytes=64)
+            row = 2 * (2 * (pair % 2) + jj) + g
+            nc.vector.tensor_tensor(
+                out=zg[s][:, jj, :, :, :],
+                in0=act[s][:, :, P * jj : P * (jj + 1), :].rearrange("p u m e -> p m u e"),
+                in1=gain_sb[0][:, row : row + 1, :, :].to_broadcast([P, P, 2, 2]),
+                op=MULT,
+            )
+
+        def quant_z(s):
+            codes = work.tile([P, 256], U32, name="zcodes", bufs=6, align_bytes=64)
+            scales = work.tile([P, 256], U8, name="zscales", bufs=6, align_bytes=64)
+            src = zg[s][:].rearrange("p jj m u e -> p (jj m u e)")
+            nc.vector.quantize_mx(out=codes[:].bitcast(FP8X4), scales=scales[:], in_=src)
+            zq[s] = (codes, scales)
+
+        def second_product(s, half):
+            pair, g = UNITS[s]
+            if True:
+                if s % 4 == 0:
+                    yb[s // 4, half] = psum.tile([P, 512], F32, name="yb", bufs=3)
+                for jj in range(2):
+                    j = 2 * (pair % 2) + jj
+                    rows = slice(P * jj, P * (jj + 1))
+                    nc.tensor.matmul_mx(
+                        out=yb[s // 4, half][:],
+                        lhsT=zq[s][0][:, rows].bitcast(FP8X4),
+                        lhsT_scale=zq[s][1][:, rows],
+                        rhs=w2w[2 * j + g][:, N * half : N * (half + 1)].bitcast(FP4X4),
+                        rhs_scale=w2s[g][:, j, 512 * half : 512 * (half + 1)],
+                        start=(s % 4 == 0 and jj == 0),
+                        stop=(s % 4 == 3 and jj == 1),
+                    )
+
+        def finish(grp, half):
+            cols = slice(512 * half, 512 * (half + 1))
+            y = work.tile([P, 512], F32, name="y", bufs=3)
+            nc.vector.tensor_tensor(out=y[:], in0=yb[grp, half][:], in1=bias[:, cols], op=ADD)
+            nc.sync.dma_start(out=out[P * grp : P * (grp + 1), cols], in_=y[:])
+
+        gain_t, gain_sb = [], []
+
+        def turn_gain():
+            gain_t.append(psum.tile([P, 2, P], F32, name="gain_t", tag="yb", bufs=3))
+            gain_words = gain_rows[:].bitcast(F32)
+            for u in range(2):
+                nc.tensor.transpose(gain_t[0][:, u, :], gain_words[:, u : 256 : 2], ident[:])
+
+        def gather_gain():
+            gain_sb.append(keep.tile([P, 8, 2, 2], BF16, name="gain_sb"))
+            nc.scalar.copy(
+                out=gain_sb[0][:].rearrange("p r u e -> p r (u e)").bitcast(F32),
+                in_=gain_t[0][:, :, 0:8].rearrange("p u r -> p r u"),
+            )
+
+        def load_xs():
+            nc.sync.dma_start(out=xs[:], in_=x_scale.rearrange("(G m j) c -> m G (j c)", m=P, j=R))
+
+        def load_gain():
+            nc.sync.dma_start(out=gain_rows[0:8, :], in_=gain.rearrange("(r f) -> r f", f=512))
+
+        def load_bias():
+            nc.sync.dma_start(out=bias[:], in_=b.partition_broadcast(P))
+
+        load_xs()
+        load_x(0, 0, 1)
+        load_x(0, 1, 2)
+        load_w1(0, 0)
+        load_w1(1, 0)
+        load_gain()
+        load_x(1)
+        load_w1(0, 1)
+        load_w1(1, 1)
+        load_x(2)
+        load_x(3)
+        load_x(4)
+        load_w2_scales(0, 0)
+        load_w2_scales(0, 1)
+        load_w2_scales(0, 2)
+        load_w2_scales(0, 3)
+        load_w2_scales(1, 0)
+        load_w2_scales(1, 1)
+        load_w2_scales(1, 2)
+        load_w2_scales(1, 3)
+        load_w2(0)
+        load_w2(2)
+        load_w2(4)
+        load_w2(6)
+        load_w2(1)
+        load_w2(3)
+        load_w2(5)
+        load_w2(7)
+        load_x(5)
+        load_x(6)
+        load_x(7)
+        load_bias()
+        widen(0, 0, 0, "V")
+        widen(0, 0, 1, "V")
+        turn(0, 0)
+        widen(0, 1, 0, "S")
+        gather(0, 0)
+        widen(0, 1, 1, "V")
+        group_w1(0, 0, 0, "V")
+        group_w1(0, 0, 1, "S")
+        group_w1(1, 0, 1, "V")
+        widen(1, 0, 0, "V")
+        widen(1, 0, 1, "S")
+        turn(0, 1)
+        widen(1, 1, 0, "V")
+        gather(0, 1)
+        quant_w1(1, 0, 1)
+        widen(1, 1, 1, "S")
+        turn(1, 0)
+        group_w1(1, 0, 0, "V")
+        group_w1(0, 1, 1, "V")
+        gather(1, 0)
+        widen(2, 0, 0, "V")
+        widen(2, 0, 1, "V")
+        group_w1(0, 1, 0, "V")
+        turn_gain()
+        gather_gain()
+        widen(2, 1, 0, "S")
+        turn(1, 1)
+        widen(2, 1, 1, "S")
+        quant_w1(0, 0, 0)
+        gather(1, 1)
+        group_w1(1, 1, 1, "S")
+        turn(2, 0)
+        quant_w1(1, 0, 0)
+        quant_x(0)
+        quant_w1(0, 1, 0)
+        quant_x(1)
+        quant_w1(0, 0, 1)
+        group_w1(1, 1, 0, "V")
+        gather(2, 0)
+        turn(2, 1)
+        gather(2, 1)
+        quant_w1(0, 1, 1)
+        quant_w1(1, 1, 0)
+        quant_w1(1, 1, 1)
+        first_product(0, 0)
+        gelu(0, 0)
+        first_product(0, 1)
+        gelu(0, 1)
+        first_product(1, 0)
+        gelu(1, 0)
+        first_product(1, 1)
+        gelu(1, 1)
+        widen(3, 0, 0, "V")
+        widen(3, 0, 1, "V")
+        widen(3, 1, 0, "V")
+        first_product(2, 0)
+        gelu(2, 0)
+        widen(3, 1, 1, "V")
+        quant_x(2)
+        first_product(2, 1)
+        gelu(2, 1)
+        apply_gain(0, 0)
+        first_product(3, 0)
+        gelu(3, 0)
+        apply_gain(0, 1)
+        turn(3, 0)
+        turn(3, 1)
+        gather(3, 0)
+        first_product(3, 1)
+        gelu(3, 1)
+        apply_gain(1, 0)
+        widen(4, 0, 0, "V")
+        quant_z(0)
+        widen(4, 0, 1, "V")
+        widen(4, 1, 0, "V")
+        gather(3, 1)
+        first_product(4, 0)
+        gelu(4, 0)
+        widen(4, 1, 1, "V")
+        apply_gain(1, 1)
+        first_product(4, 1)
+        gelu(4, 1)
+        apply_gain(2, 0)
+        quant_z(1)
+        second_product(0, 0)
+        first_product(5, 0)
+        gelu(5, 0)
+        apply_gain(2, 1)
+        turn(4, 0)
+        turn(4, 1)
+        quant_x(3)
+        gather(4, 0)
+        first_product(5, 1)
+        gelu(5, 1)
+        apply_gain(3, 0)
+        widen(5, 0, 0, "V")
+        second_product(0, 1)
+        quant_z(2)
+        widen(5, 0, 1, "V")
+        widen(5, 1, 0, "V")
+        gather(4, 1)
+        second_product(1, 0)
+        first_product(6, 0)
+        gelu(6, 0)
+        widen(5, 1, 1, "V")
+        apply_gain(3, 1)
+        first_product(6, 1)
+        gelu(6, 1)
+        apply_gain(4, 0)
+        second_product(1, 1)
+        quant_z(3)
+        second_product(2, 0)
+        first_product(7, 0)
+        gelu(7, 0)
+        apply_gain(4, 1)
+        turn(5, 0)
+        turn(5, 1)
+        quant_x(4)
+        gather(5, 0)
+        first_product(7, 1)
+        gelu(7, 1)
+        apply_gain(5, 0)
+        widen(6, 0, 0, "V")
+        second_product(2, 1)
+        quant_z(4)
+        widen(6, 0, 1, "V")
+        widen(6, 1, 0, "V")
+        gather(5, 1)
+        second_product(3, 0)
+        first_product(8, 0)
+        gelu(8, 0)
+        widen(6, 1, 1, "V")
+        apply_gain(5, 1)
+        first_product(8, 1)
+        gelu(8, 1)
+        apply_gain(6, 0)
+        second_product(3, 1)
+        quant_z(5)
+        finish(0, 0)
+        second_product(4, 0)
+        first_product(9, 0)
+        gelu(9, 0)
+        apply_gain(6, 1)
+        turn(6, 0)
+        turn(6, 1)
+        quant_x(5)
+        gather(6, 0)
+        first_product(9, 1)
+        gelu(9, 1)
+        apply_gain(7, 0)
+        widen(7, 0, 0, "V")
+        second_product(4, 1)
+        quant_z(6)
+        widen(7, 0, 1, "V")
+        widen(7, 1, 0, "V")
+        gather(6, 1)
+        second_product(5, 0)
+        first_product(10, 0)
+        gelu(10, 0)
+        widen(7, 1, 1, "V")
+        apply_gain(7, 1)
+        first_product(10, 1)
+        gelu(10, 1)
+        apply_gain(8, 0)
+        second_product(5, 1)
+        quant_z(7)
+        second_product(6, 0)
+        first_product(11, 0)
+        gelu(11, 0)
+        apply_gain(8, 1)
+        turn(7, 0)
+        turn(7, 1)
+        quant_x(6)
+        gather(7, 0)
+        first_product(11, 1)
+        gelu(11, 1)
+        apply_gain(9, 0)
+        second_product(6, 1)
+        quant_z(8)
+        finish(0, 1)
+        gather(7, 1)
+        second_product(7, 0)
+        first_product(12, 0)
+        gelu(12, 0)
+        apply_gain(9, 1)
+        first_product(12, 1)
+        gelu(12, 1)
+        apply_gain(10, 0)
+        second_product(7, 1)
+        quant_z(9)
+        finish(1, 0)
+        second_product(8, 0)
+        first_product(13, 0)
+        gelu(13, 0)
+        apply_gain(10, 1)
+        quant_x(7)
+        first_product(13, 1)
+        gelu(13, 1)
+        apply_gain(11, 0)
+        second_product(8, 1)
+        quant_z(10)
+        second_product(9, 0)
+        first_product(14, 0)
+        gelu(14, 0)
+        apply_gain(11, 1)
+        first_product(14, 1)
+        gelu(14, 1)
+        apply_gain(12, 0)
+        second_product(9, 1)
+        quant_z(11)
+        second_product(10, 0)
+        first_product(15, 0)
+        gelu(15, 0)
+        apply_gain(12, 1)
+        first_product(15, 1)
+        gelu(15, 1)
+        apply_gain(13, 0)
+        second_product(10, 1)
+        quant_z(12)
+        finish(1, 1)
+        second_product(11, 0)
+        apply_gain(13, 1)
+        apply_gain(14, 0)
+        second_product(11, 1)
+        quant_z(13)
+        finish(2, 0)
+        second_product(12, 0)
+        apply_gain(14, 1)
+        apply_gain(15, 0)
+        second_product(12, 1)
+        quant_z(14)
+        second_product(13, 0)
+        apply_gain(15, 1)
+        second_product(13, 1)
+        quant_z(15)
+        second_product(14, 0)
+        second_product(14, 1)
+        finish(2, 1)
+        second_product(15, 0)
+        second_product(15, 1)
+        finish(3, 0)
+        finish(3, 1)

@@ -22,7 +22,7 @@ GELU = mybir.ActivationFunctionType.Gelu_apprx_tanh
 P = 128
 GROUPS = 4
 PAIRS = 8
-XW_BUFS = 10
+XW_BUFS = 24
 UNITS = [(0, 0), (1, 0), (0, 1), (1, 1)] + [(pair, g) for pair in range(2, PAIRS) for g in range(2)]
 
 
@@ -46,7 +46,9 @@ def tile_image_token_merger_d4_kernel(tc, x_bytes, x_scale, w1, gain, w2_words, 
         for g in range(2):
             nc.vector.memset(w2s[g][:].rearrange("p j n -> p (j n)").bitcast(I32), 0)
 
-        xs = keep.tile([P, GROUPS, 32], F32, name="xs")
+        ident16 = keep.tile([P, P], BF16, name="ident16")
+        nc.vector.tensor_copy(out=ident16[:], in_=ident[:])
+        xs = [keep.tile([P, 1, 32], F32, name="xs0"), keep.tile([P, GROUPS - 1, 32], F32, name="xs1")]
         xb = [keep.tile([P, 2 * K], U8, name="xb%d" % i) for i in range(PAIRS)]
         w1raw = [[keep.tile([P, 4, 512], BF16, name="w1raw%d%d" % (c, g)) for g in range(2)] for c in range(2)]
         w2w = [keep.tile([P, 2 * N], U8, name="w2w%d" % i, align_bytes=64) for i in range(8)]
@@ -71,7 +73,7 @@ def tile_image_token_merger_d4_kernel(tc, x_bytes, x_scale, w1, gain, w2_words, 
         def load_w2(i):
             nc.sync.dma_start(out=w2w[i][:].bitcast(I32), in_=w2_words[i].bitcast(I32))
 
-        modes = {}
+        modes, w1t = {}, {}
         xw, xt, xg, xq, w1g, w1q, hb, act, zg, zq, yb = {}, {}, {}, {}, {}, {}, {}, {}, {}, {}, {}
 
         def widen(pair, jj, c, mode):
@@ -84,7 +86,7 @@ def tile_image_token_merger_d4_kernel(tc, x_bytes, x_scale, w1, gain, w2_words, 
                 blk = 4 * c + q
                 col = 8 * (2 * (pair % 2) + jj) + blk
                 src = xb[pair][:, K * jj + 128 * blk : K * jj + 128 * (blk + 1)].bitcast(FP8)
-                scale = xs[:, pair // 2, col : col + 1]
+                scale = xs[0][:, 0, col : col + 1] if pair < 2 else xs[1][:, pair // 2 - 1, col : col + 1]
                 if mode == "V":
                     nc.vector.tensor_scalar(
                         out=dst[:].rearrange("m (u p e) -> m p u e", u=2, e=2)[:, 32 * q : 32 * (q + 1), :, :],
@@ -102,7 +104,7 @@ def tile_image_token_merger_d4_kernel(tc, x_bytes, x_scale, w1, gain, w2_words, 
                 )
 
         def turn(pair, jj):
-            xt[pair, jj] = psum.tile([P, 2, 2, P], F32, name="xt", bufs=2)
+            xt[pair, jj] = psum.tile([P, 2, 2, P], F32, name="xt", tag="ring", bufs=6)
             for c in range(2):
                 words = xw[pair, jj, c][:].bitcast(F32)
                 for u in range(2):
@@ -111,23 +113,35 @@ def tile_image_token_merger_d4_kernel(tc, x_bytes, x_scale, w1, gain, w2_words, 
 
         def gather(pair, jj):
             if pair not in xg:
-                xg[pair] = work.tile([P, 2, 2, P, 2], F32, name="xg", bufs=3, align_bytes=64)
+                xg[pair] = work.tile([P, 2, 2, P, 2], F32, name="xg", bufs=5, align_bytes=64)
             nc.scalar.copy(out=xg[pair][:, :, jj, :, :], in_=xt[pair, jj][:].rearrange("p c u m -> p c m u"))
 
         def quant_x(pair):
-            codes = work.tile([P, 512], U32, name="xcodes", bufs=4, align_bytes=64)
-            scales = work.tile([P, 512], U8, name="xscales", bufs=4, align_bytes=64)
+            codes = work.tile([P, 512], U32, name="xcodes", bufs=6, align_bytes=64)
+            scales = work.tile([P, 512], U8, name="xscales", bufs=6, align_bytes=64)
             src = xg[pair][:].rearrange("p c jj m u -> p (c jj m u)").bitcast(BF16)
             nc.vector.quantize_mx(out=codes[:].bitcast(FP8X4), scales=scales[:], in_=src)
             xq[pair] = (codes, scales)
 
         def group_w1(c, g, u, mode):
             w1g[c, g, u] = keep.tile([P, 2, P, 4], BF16, name="w1g%d%d%d" % (c, g, u), align_bytes=64)
+            if mode == "P":
+                w1t[c, g, u] = psum.tile([P, 2, P, 4], BF16, name="w1t", tag="yb", bufs=2)
+                src = w1raw[c][g][:].rearrange("p s (m t) -> p m s t", t=4)[:, :, :, 2 * u : 2 * u + 2]
+                dst = w1t[c, g, u][:].rearrange("p t m s -> p m s t")
+                for mh in range(2):
+                    rows = slice(64 * mh, 64 * (mh + 1))
+                    nc.tensor.matmul(out=dst[:, rows], lhsT=ident16[:], rhs=src[:, rows], start=True, stop=True)
+                return
             copy = nc.vector.tensor_copy if mode == "V" else nc.scalar.copy
             copy(
                 out=w1g[c, g, u][:].rearrange("p t m s -> p m s t"),
                 in_=w1raw[c][g][:].rearrange("p s (m t) -> p m s t", t=4)[:, :, :, 2 * u : 2 * u + 2],
             )
+
+        def drain_w1(c, g, u, mode):
+            copy = nc.vector.tensor_copy if mode == "V" else nc.scalar.copy
+            copy(out=w1g[c, g, u][:], in_=w1t[c, g, u][:])
 
         def quant_w1(c, g, u):
             codes = keep.tile([P, 256], U32, name="w1codes%d%d%d" % (c, g, u), align_bytes=64)
@@ -138,7 +152,7 @@ def tile_image_token_merger_d4_kernel(tc, x_bytes, x_scale, w1, gain, w2_words, 
 
         def first_product(s, u):
             pair, g = UNITS[s]
-            hb[s, u] = psum.tile([P, 2, 256], F32, name="hb", bufs=3)
+            hb[s, u] = psum.tile([P, 2, 256], F32, name="hb", tag="ring", bufs=6)
             for e in range(2):
                 cols = slice(P * e, P * (e + 1))
                 for c in range(2):
@@ -155,7 +169,7 @@ def tile_image_token_merger_d4_kernel(tc, x_bytes, x_scale, w1, gain, w2_words, 
 
         def gelu(s, u):
             if s not in act:
-                act[s] = work.tile([P, 2, 256, 2], F32, name="act", bufs=6)
+                act[s] = work.tile([P, 2, 256, 2], F32, name="act", bufs=7)
             nc.scalar.activation(out=act[s][:, u, :, :], in_=hb[s, u][:].rearrange("p e n -> p n e"), func=GELU)
 
         def apply_gain(s, jj):
@@ -177,11 +191,37 @@ def tile_image_token_merger_d4_kernel(tc, x_bytes, x_scale, w1, gain, w2_words, 
             nc.vector.quantize_mx(out=codes[:].bitcast(FP8X4), scales=scales[:], in_=src)
             zq[s] = (codes, scales)
 
+        def quant_z_last(s, jj):
+            codes = work.tile([P, P], U32, name="lcodes", bufs=2, align_bytes=64)
+            scales = work.tile([P, P], U8, name="lscales", bufs=2, align_bytes=64)
+            src = zg[s][:, jj].rearrange("p m u e -> p (m u e)")
+            nc.vector.quantize_mx(out=codes[:].bitcast(FP8X4), scales=scales[:], in_=src)
+            zq[s, jj] = (codes, scales)
+
+        def second_last(s, jj, half):
+            pair, g = UNITS[s]
+            j = 2 * (pair % 2) + jj
+            nc.tensor.matmul_mx(
+                out=yb[s // 4, half][:],
+                lhsT=zq[s, jj][0][:].bitcast(FP8X4),
+                lhsT_scale=zq[s, jj][1][:],
+                rhs=w2w[2 * j + g][:, N * half : N * (half + 1)].bitcast(FP4X4),
+                rhs_scale=w2s[g][:, j, 512 * half : 512 * (half + 1)],
+                start=False,
+                stop=(jj == 1),
+            )
+
+        def finish_last(grp, half, q):
+            cols = slice(512 * half + 256 * q, 512 * half + 256 * (q + 1))
+            y = work.tile([P, 256], F32, name="ylast", bufs=4)
+            nc.vector.tensor_tensor(out=y[:], in0=yb[grp, half][:, 256 * q : 256 * (q + 1)], in1=bias[:, cols], op=ADD)
+            nc.sync.dma_start(out=out[P * grp : P * (grp + 1), cols], in_=y[:])
+
         def second_product(s, half):
             pair, g = UNITS[s]
             if True:
                 if s % 4 == 0:
-                    yb[s // 4, half] = psum.tile([P, 512], F32, name="yb", bufs=3)
+                    yb[s // 4, half] = psum.tile([P, 512], F32, name="yb", bufs=2)
                 for jj in range(2):
                     j = 2 * (pair % 2) + jj
                     rows = slice(P * jj, P * (jj + 1))
@@ -204,7 +244,7 @@ def tile_image_token_merger_d4_kernel(tc, x_bytes, x_scale, w1, gain, w2_words, 
         gain_t, gain_sb = [], []
 
         def turn_gain():
-            gain_t.append(psum.tile([P, 2, P], F32, name="gain_t", tag="yb", bufs=3))
+            gain_t.append(psum.tile([P, 2, P], F32, name="gain_t", tag="yb", bufs=2))
             gain_words = gain_rows[:].bitcast(F32)
             for u in range(2):
                 nc.tensor.transpose(gain_t[0][:, u, :], gain_words[:, u : 256 : 2], ident[:])
@@ -216,8 +256,9 @@ def tile_image_token_merger_d4_kernel(tc, x_bytes, x_scale, w1, gain, w2_words, 
                 in_=gain_t[0][:, :, 0:8].rearrange("p u r -> p r u"),
             )
 
-        def load_xs():
-            nc.sync.dma_start(out=xs[:], in_=x_scale.rearrange("(G m j) c -> m G (j c)", m=P, j=R))
+        def load_xs(i):
+            rows = x_scale.rearrange("(G m j) c -> m G (j c)", m=P, j=R)
+            nc.sync.dma_start(out=xs[i][:], in_=rows[:, 0:1, :] if i == 0 else rows[:, 1:GROUPS, :])
 
         def load_gain():
             nc.sync.dma_start(out=gain_rows[0:8, :], in_=gain.rearrange("(r f) -> r f", f=512))
@@ -225,26 +266,57 @@ def tile_image_token_merger_d4_kernel(tc, x_bytes, x_scale, w1, gain, w2_words, 
         def load_bias():
             nc.sync.dma_start(out=bias[:], in_=b.partition_broadcast(P))
 
-        load_xs()
         load_x(0, 0, 1)
+        load_xs(0)
         load_x(0, 1, 2)
-        load_w1(0, 0)
-        load_w1(1, 0)
-        load_gain()
         load_x(1)
-        load_w1(0, 1)
-        load_w1(1, 1)
         load_x(2)
+        load_xs(1)
         load_x(3)
+        load_w1(1, 0)
         load_x(4)
-        load_w2_scales(0, 0)
-        load_w2_scales(0, 1)
-        load_w2_scales(0, 2)
-        load_w2_scales(0, 3)
-        load_w2_scales(1, 0)
-        load_w2_scales(1, 1)
-        load_w2_scales(1, 2)
-        load_w2_scales(1, 3)
+        load_w1(0, 0)
+        load_x(5)
+        load_w1(0, 1)
+        widen(0, 0, 0, "V")
+        widen(0, 0, 1, "S")
+        widen(0, 1, 0, "V")
+        widen(0, 1, 1, "V")
+        widen(1, 0, 0, "S")
+        widen(1, 0, 1, "V")
+        widen(1, 1, 0, "V")
+        widen(1, 1, 1, "S")
+        widen(2, 0, 0, "S")
+        widen(2, 0, 1, "S")
+        widen(2, 1, 0, "V")
+        widen(2, 1, 1, "V")
+        widen(3, 0, 0, "V")
+        widen(3, 0, 1, "S")
+        widen(3, 1, 0, "V")
+        turn(0, 0)
+        widen(3, 1, 1, "V")
+        widen(4, 0, 0, "V")
+        widen(4, 0, 1, "V")
+        widen(4, 1, 0, "S")
+        gather(0, 0)
+        widen(4, 1, 1, "V")
+        turn(0, 1)
+        load_x(6)
+        group_w1(0, 0, 0, "V")
+        gather(0, 1)
+        turn(1, 0)
+        load_gain()
+        load_w1(1, 1)
+        load_x(7)
+        group_w1(1, 0, 0, "P")
+        gather(1, 0)
+        turn(1, 1)
+        drain_w1(1, 0, 0, "S")
+        group_w1(0, 0, 1, "V")
+        quant_x(0)
+        gather(1, 1)
+        turn(2, 0)
+        group_w1(1, 0, 1, "S")
         load_w2(0)
         load_w2(2)
         load_w2(4)
@@ -253,54 +325,43 @@ def tile_image_token_merger_d4_kernel(tc, x_bytes, x_scale, w1, gain, w2_words, 
         load_w2(3)
         load_w2(5)
         load_w2(7)
-        load_x(5)
-        load_x(6)
-        load_x(7)
-        load_bias()
-        widen(0, 0, 0, "V")
-        widen(0, 0, 1, "V")
-        turn(0, 0)
-        widen(0, 1, 0, "S")
-        gather(0, 0)
-        widen(0, 1, 1, "V")
-        group_w1(0, 0, 0, "V")
-        group_w1(0, 0, 1, "S")
-        group_w1(1, 0, 1, "V")
-        widen(1, 0, 0, "V")
-        widen(1, 0, 1, "S")
-        turn(0, 1)
-        widen(1, 1, 0, "V")
-        gather(0, 1)
-        quant_w1(1, 0, 1)
-        widen(1, 1, 1, "S")
-        turn(1, 0)
-        group_w1(1, 0, 0, "V")
-        group_w1(0, 1, 1, "V")
-        gather(1, 0)
-        widen(2, 0, 0, "V")
-        widen(2, 0, 1, "V")
-        group_w1(0, 1, 0, "V")
-        turn_gain()
-        gather_gain()
-        widen(2, 1, 0, "S")
-        turn(1, 1)
-        widen(2, 1, 1, "S")
-        quant_w1(0, 0, 0)
-        gather(1, 1)
-        group_w1(1, 1, 1, "S")
-        turn(2, 0)
-        quant_w1(1, 0, 0)
-        quant_x(0)
-        quant_w1(0, 1, 0)
-        quant_x(1)
-        quant_w1(0, 0, 1)
-        group_w1(1, 1, 0, "V")
         gather(2, 0)
+        group_w1(0, 1, 0, "V")
         turn(2, 1)
+        quant_w1(0, 0, 0)
+        load_w2_scales(0, 0)
+        load_w2_scales(0, 1)
+        load_w2_scales(0, 2)
+        load_w2_scales(0, 3)
+        load_w2_scales(1, 0)
+        load_w2_scales(1, 1)
+        load_w2_scales(1, 2)
+        load_w2_scales(1, 3)
+        quant_w1(1, 0, 0)
+        group_w1(1, 1, 0, "V")
         gather(2, 1)
-        quant_w1(0, 1, 1)
+        turn(3, 0)
+        quant_w1(0, 0, 1)
+        group_w1(0, 1, 1, "P")
+        gather(3, 0)
+        quant_w1(1, 0, 1)
+        turn(3, 1)
+        drain_w1(0, 1, 1, "S")
+        quant_x(1)
+        group_w1(1, 1, 1, "V")
+        gather(3, 1)
+        turn(4, 0)
+        quant_w1(0, 1, 0)
         quant_w1(1, 1, 0)
+        load_bias()
+        quant_w1(0, 1, 1)
         quant_w1(1, 1, 1)
+        gather(4, 0)
+        turn(4, 1)
+        turn_gain()
+        gather(4, 1)
+        gather_gain()
+        quant_x(3)
         first_product(0, 0)
         gelu(0, 0)
         first_product(0, 1)
@@ -309,193 +370,181 @@ def tile_image_token_merger_d4_kernel(tc, x_bytes, x_scale, w1, gain, w2_words, 
         gelu(1, 0)
         first_product(1, 1)
         gelu(1, 1)
-        widen(3, 0, 0, "V")
-        widen(3, 0, 1, "V")
-        widen(3, 1, 0, "V")
+        quant_x(2)
         first_product(2, 0)
         gelu(2, 0)
-        widen(3, 1, 1, "V")
-        quant_x(2)
         first_product(2, 1)
         gelu(2, 1)
-        apply_gain(0, 0)
+        quant_x(4)
         first_product(3, 0)
         gelu(3, 0)
-        apply_gain(0, 1)
-        turn(3, 0)
-        turn(3, 1)
-        gather(3, 0)
         first_product(3, 1)
         gelu(3, 1)
-        apply_gain(1, 0)
-        widen(4, 0, 0, "V")
-        quant_z(0)
-        widen(4, 0, 1, "V")
-        widen(4, 1, 0, "V")
-        gather(3, 1)
         first_product(4, 0)
         gelu(4, 0)
-        widen(4, 1, 1, "V")
-        apply_gain(1, 1)
         first_product(4, 1)
         gelu(4, 1)
-        apply_gain(2, 0)
-        quant_z(1)
-        second_product(0, 0)
+        apply_gain(0, 0)
+        apply_gain(0, 1)
         first_product(5, 0)
         gelu(5, 0)
-        apply_gain(2, 1)
-        turn(4, 0)
-        turn(4, 1)
-        quant_x(3)
-        gather(4, 0)
         first_product(5, 1)
         gelu(5, 1)
-        apply_gain(3, 0)
-        widen(5, 0, 0, "V")
-        second_product(0, 1)
-        quant_z(2)
-        widen(5, 0, 1, "V")
-        widen(5, 1, 0, "V")
-        gather(4, 1)
-        second_product(1, 0)
+        apply_gain(1, 0)
+        quant_z(0)
+        apply_gain(1, 1)
+        apply_gain(2, 0)
         first_product(6, 0)
         gelu(6, 0)
-        widen(5, 1, 1, "V")
-        apply_gain(3, 1)
         first_product(6, 1)
         gelu(6, 1)
-        apply_gain(4, 0)
-        second_product(1, 1)
-        quant_z(3)
-        second_product(2, 0)
+        quant_z(1)
+        second_product(0, 0)
+        apply_gain(2, 1)
+        second_product(0, 1)
+        apply_gain(3, 0)
+        quant_z(2)
         first_product(7, 0)
         gelu(7, 0)
-        apply_gain(4, 1)
-        turn(5, 0)
-        turn(5, 1)
-        quant_x(4)
-        gather(5, 0)
         first_product(7, 1)
         gelu(7, 1)
-        apply_gain(5, 0)
+        second_product(1, 0)
+        widen(5, 0, 0, "V")
+        widen(5, 0, 1, "S")
+        widen(5, 1, 0, "V")
+        widen(5, 1, 1, "S")
         widen(6, 0, 0, "V")
-        second_product(2, 1)
-        quant_z(4)
         widen(6, 0, 1, "V")
-        widen(6, 1, 0, "V")
-        gather(5, 1)
-        second_product(3, 0)
-        first_product(8, 0)
-        gelu(8, 0)
+        widen(6, 1, 0, "S")
         widen(6, 1, 1, "V")
-        apply_gain(5, 1)
-        first_product(8, 1)
-        gelu(8, 1)
-        apply_gain(6, 0)
-        second_product(3, 1)
-        quant_z(5)
-        finish(0, 0)
-        second_product(4, 0)
-        first_product(9, 0)
-        gelu(9, 0)
-        apply_gain(6, 1)
-        turn(6, 0)
-        turn(6, 1)
-        quant_x(5)
-        gather(6, 0)
-        first_product(9, 1)
-        gelu(9, 1)
-        apply_gain(7, 0)
         widen(7, 0, 0, "V")
-        second_product(4, 1)
-        quant_z(6)
         widen(7, 0, 1, "V")
         widen(7, 1, 0, "V")
-        gather(6, 1)
-        second_product(5, 0)
-        first_product(10, 0)
-        gelu(10, 0)
         widen(7, 1, 1, "V")
-        apply_gain(7, 1)
-        first_product(10, 1)
-        gelu(10, 1)
-        apply_gain(8, 0)
-        second_product(5, 1)
-        quant_z(7)
-        second_product(6, 0)
-        first_product(11, 0)
-        gelu(11, 0)
-        apply_gain(8, 1)
+        apply_gain(3, 1)
+        second_product(1, 1)
+        apply_gain(4, 0)
+        quant_z(3)
+        second_product(2, 0)
+        first_product(8, 0)
+        gelu(8, 0)
+        first_product(8, 1)
+        gelu(8, 1)
+        apply_gain(4, 1)
+        second_product(2, 1)
+        turn(5, 0)
+        turn(5, 1)
+        turn(6, 0)
+        turn(6, 1)
         turn(7, 0)
         turn(7, 1)
-        quant_x(6)
+        apply_gain(5, 0)
+        gather(5, 0)
+        gather(5, 1)
+        gather(6, 0)
+        quant_z(4)
+        gather(6, 1)
+        second_product(3, 0)
         gather(7, 0)
+        gather(7, 1)
+        apply_gain(5, 1)
+        second_product(3, 1)
+        first_product(9, 0)
+        gelu(9, 0)
+        first_product(9, 1)
+        gelu(9, 1)
+        apply_gain(6, 0)
+        quant_x(5)
+        finish(0, 0)
+        quant_z(5)
+        second_product(4, 0)
+        finish(0, 1)
+        apply_gain(6, 1)
+        apply_gain(7, 0)
+        first_product(10, 0)
+        gelu(10, 0)
+        first_product(10, 1)
+        gelu(10, 1)
+        quant_z(6)
+        quant_x(6)
+        second_product(4, 1)
+        second_product(5, 0)
+        apply_gain(7, 1)
+        apply_gain(8, 0)
+        quant_z(7)
+        first_product(11, 0)
+        gelu(11, 0)
         first_product(11, 1)
         gelu(11, 1)
+        second_product(5, 1)
+        second_product(6, 0)
+        apply_gain(8, 1)
         apply_gain(9, 0)
-        second_product(6, 1)
         quant_z(8)
-        finish(0, 1)
-        gather(7, 1)
+        second_product(6, 1)
         second_product(7, 0)
         first_product(12, 0)
         gelu(12, 0)
-        apply_gain(9, 1)
         first_product(12, 1)
         gelu(12, 1)
+        apply_gain(9, 1)
         apply_gain(10, 0)
-        second_product(7, 1)
-        quant_z(9)
         finish(1, 0)
+        quant_z(9)
+        second_product(7, 1)
         second_product(8, 0)
+        quant_x(7)
+        apply_gain(10, 1)
         first_product(13, 0)
         gelu(13, 0)
-        apply_gain(10, 1)
-        quant_x(7)
         first_product(13, 1)
         gelu(13, 1)
         apply_gain(11, 0)
-        second_product(8, 1)
+        finish(1, 1)
         quant_z(10)
         second_product(9, 0)
+        second_product(8, 1)
+        apply_gain(11, 1)
+        apply_gain(12, 0)
         first_product(14, 0)
         gelu(14, 0)
-        apply_gain(11, 1)
         first_product(14, 1)
         gelu(14, 1)
-        apply_gain(12, 0)
-        second_product(9, 1)
         quant_z(11)
         second_product(10, 0)
+        second_product(9, 1)
+        apply_gain(12, 1)
+        apply_gain(13, 0)
+        quant_z(12)
+        second_product(11, 0)
         first_product(15, 0)
         gelu(15, 0)
-        apply_gain(12, 1)
         first_product(15, 1)
         gelu(15, 1)
-        apply_gain(13, 0)
         second_product(10, 1)
-        quant_z(12)
-        finish(1, 1)
-        second_product(11, 0)
         apply_gain(13, 1)
         apply_gain(14, 0)
-        second_product(11, 1)
-        quant_z(13)
         finish(2, 0)
+        quant_z(13)
         second_product(12, 0)
+        second_product(11, 1)
         apply_gain(14, 1)
         apply_gain(15, 0)
-        second_product(12, 1)
-        quant_z(14)
         second_product(13, 0)
-        apply_gain(15, 1)
-        second_product(13, 1)
-        quant_z(15)
-        second_product(14, 0)
-        second_product(14, 1)
+        quant_z(14)
         finish(2, 1)
-        second_product(15, 0)
-        second_product(15, 1)
-        finish(3, 0)
-        finish(3, 1)
+        apply_gain(15, 1)
+        second_product(14, 0)
+        quant_z_last(15, 1)
+        quant_z_last(15, 0)
+        second_product(12, 1)
+        second_product(13, 1)
+        second_product(14, 1)
+        second_last(15, 0, 1)
+        second_last(15, 1, 1)
+        finish_last(3, 1, 0)
+        finish_last(3, 1, 1)
+        second_last(15, 0, 0)
+        second_last(15, 1, 0)
+        finish_last(3, 0, 0)
+        finish_last(3, 0, 1)

@@ -46,23 +46,26 @@ def tile_image_token_merger_d4_kernel(tc, x_bytes, x_scale, w1, gain, w2_words, 
         for g in range(2):
             nc.vector.memset(w2s[g][:].rearrange("p j n -> p (j n)").bitcast(I32), 0)
 
-        ident16 = keep.tile([P, P], BF16, name="ident16")
-        nc.vector.tensor_copy(out=ident16[:], in_=ident[:])
         xs = [keep.tile([P, 1, 32], F32, name="xs0"), keep.tile([P, GROUPS - 1, 32], F32, name="xs1")]
-        xb = [keep.tile([P, 2 * K], U8, name="xb%d" % i) for i in range(PAIRS)]
-        w1raw = [[keep.tile([P, 4, 512], BF16, name="w1raw%d%d" % (c, g)) for g in range(2)] for c in range(2)]
+        xb = [keep.tile([P, R * K], U8, name="xb%d" % i) for i in range(GROUPS)]
+        w1raw = [keep.tile([P, 4, F], BF16, name="w1raw%d" % c) for c in range(2)]
         w2w = [keep.tile([P, 2 * N], U8, name="w2w%d" % i, align_bytes=64) for i in range(8)]
         bias = keep.tile([P, N], BF16, name="bias")
-        x_rows = x_bytes.rearrange("(G m i jj) k -> G i m (jj k)", m=P, i=2, jj=2)
+        x_rows = x_bytes.rearrange("(G m j) k -> G m (j k)", m=P, j=R)
         w1_rows = w1.rearrange("(c p s) f -> c p s f", p=P, s=4)
         w2s_rows = w2_scales.rearrange("(j g) r n -> g r j n", g=2)
 
-        def load_x(pair, lo=0, hi=2):
+        def load_x(grp, lo, hi):
             cols = slice(K * lo, K * hi)
-            nc.sync.dma_start(out=xb[pair][:, cols], in_=x_rows[pair // 2, pair % 2][:, cols])
+            nc.sync.dma_start(out=xb[grp][:, cols], in_=x_rows[grp][:, cols])
 
-        def load_w1(c, g):
-            nc.sync.dma_start(out=w1raw[c][g][:], in_=w1_rows[c, :, :, 512 * g : 512 * (g + 1)])
+        def load_w1(c):
+            nc.sync.dma_start(out=w1raw[c][:], in_=w1_rows[c])
+
+        def warm_up():
+            if not scratch:
+                scratch.append(psum.tile([P, 512], F32, name="scratch", tag="yb", bufs=2))
+            nc.tensor.matmul(out=scratch[0][:], lhsT=gain_rows[:, 0:P], rhs=gain_rows[:], start=True, stop=True)
 
         def load_w2_scales(g, q):
             nc.sync.dma_start(
@@ -73,7 +76,7 @@ def tile_image_token_merger_d4_kernel(tc, x_bytes, x_scale, w1, gain, w2_words, 
         def load_w2(i):
             nc.sync.dma_start(out=w2w[i][:].bitcast(I32), in_=w2_words[i].bitcast(I32))
 
-        modes, w1t = {}, {}
+        modes, scratch = {}, []
         xw, xt, xg, xq, w1g, w1q, hb, act, zg, zq, yb = {}, {}, {}, {}, {}, {}, {}, {}, {}, {}, {}
 
         def widen(pair, jj, c, mode):
@@ -85,7 +88,7 @@ def tile_image_token_merger_d4_kernel(tc, x_bytes, x_scale, w1, gain, w2_words, 
             for q in range(4):
                 blk = 4 * c + q
                 col = 8 * (2 * (pair % 2) + jj) + blk
-                src = xb[pair][:, K * jj + 128 * blk : K * jj + 128 * (blk + 1)].bitcast(FP8)
+                src = xb[pair // 2][:, 128 * col : 128 * (col + 1)].bitcast(FP8)
                 scale = xs[0][:, 0, col : col + 1] if pair < 2 else xs[1][:, pair // 2 - 1, col : col + 1]
                 if mode == "V":
                     nc.vector.tensor_scalar(
@@ -94,6 +97,10 @@ def tile_image_token_merger_d4_kernel(tc, x_bytes, x_scale, w1, gain, w2_words, 
                         scalar1=scale,
                         scalar2=None,
                         op0=MULT,
+                    )
+                elif mode == "N":
+                    nc.vector.tensor_scalar(
+                        out=dst[:, 128 * q : 128 * (q + 1)], in0=src, scalar1=scale, scalar2=None, op0=MULT
                     )
                 else:
                     nc.scalar.activation(out=dst[:, 128 * q : 128 * (q + 1)], in_=src, func=COPY, scale=scale)
@@ -108,7 +115,7 @@ def tile_image_token_merger_d4_kernel(tc, x_bytes, x_scale, w1, gain, w2_words, 
             for c in range(2):
                 words = xw[pair, jj, c][:].bitcast(F32)
                 for u in range(2):
-                    src = words[:, u : 256 : 2] if modes[pair, jj, c] == "S" else words[:, P * u : P * (u + 1)]
+                    src = words[:, u : 256 : 2] if modes[pair, jj, c] in ("S", "N") else words[:, P * u : P * (u + 1)]
                     nc.tensor.transpose(xt[pair, jj][:, c, u, :], src, ident[:])
 
         def gather(pair, jj):
@@ -123,30 +130,20 @@ def tile_image_token_merger_d4_kernel(tc, x_bytes, x_scale, w1, gain, w2_words, 
             nc.vector.quantize_mx(out=codes[:].bitcast(FP8X4), scales=scales[:], in_=src)
             xq[pair] = (codes, scales)
 
-        def group_w1(c, g, u, mode):
-            w1g[c, g, u] = keep.tile([P, 2, P, 4], BF16, name="w1g%d%d%d" % (c, g, u), align_bytes=64)
-            if mode == "P":
-                w1t[c, g, u] = psum.tile([P, 2, P, 4], BF16, name="w1t", tag="yb", bufs=2)
-                src = w1raw[c][g][:].rearrange("p s (m t) -> p m s t", t=4)[:, :, :, 2 * u : 2 * u + 2]
-                dst = w1t[c, g, u][:].rearrange("p t m s -> p m s t")
-                for mh in range(2):
-                    rows = slice(64 * mh, 64 * (mh + 1))
-                    nc.tensor.matmul(out=dst[:, rows], lhsT=ident16[:], rhs=src[:, rows], start=True, stop=True)
-                return
+        def group_w1(c, g, mh, mode):
+            if (c, g) not in w1g:
+                w1g[c, g] = keep.tile([P, 4, P, 4], BF16, name="w1g%d%d" % (c, g), align_bytes=64)
             copy = nc.vector.tensor_copy if mode == "V" else nc.scalar.copy
+            part = slice(32 * mh, 32 * (mh + 1))
             copy(
-                out=w1g[c, g, u][:].rearrange("p t m s -> p m s t"),
-                in_=w1raw[c][g][:].rearrange("p s (m t) -> p m s t", t=4)[:, :, :, 2 * u : 2 * u + 2],
+                out=w1g[c, g][:].rearrange("p t (a m) s -> p a t m s", m=2)[:, part],
+                in_=w1raw[c][:, :, 512 * g : 512 * (g + 1)].rearrange("p s (a m t) -> p a t m s", m=2, t=4)[:, part],
             )
-
-        def drain_w1(c, g, u, mode):
-            copy = nc.vector.tensor_copy if mode == "V" else nc.scalar.copy
-            copy(out=w1g[c, g, u][:], in_=w1t[c, g, u][:])
 
         def quant_w1(c, g, u):
             codes = keep.tile([P, 256], U32, name="w1codes%d%d%d" % (c, g, u), align_bytes=64)
             scales = keep.tile([P, 256], U8, name="w1scales%d%d%d" % (c, g, u), align_bytes=64)
-            src = w1g[c, g, u][:].rearrange("p t m s -> p (t m s)")
+            src = w1g[c, g][:, 2 * u : 2 * u + 2].rearrange("p t m s -> p (t m s)")
             nc.vector.quantize_mx(out=codes[:].bitcast(FP8X4), scales=scales[:], in_=src)
             w1q[c, g, u] = (codes, scales)
 
@@ -269,54 +266,28 @@ def tile_image_token_merger_d4_kernel(tc, x_bytes, x_scale, w1, gain, w2_words, 
         load_x(0, 0, 1)
         load_xs(0)
         load_x(0, 1, 2)
-        load_x(1)
-        load_x(2)
+        load_x(0, 2, 4)
+        load_x(1, 0, 4)
         load_xs(1)
-        load_x(3)
-        load_w1(1, 0)
-        load_x(4)
-        load_w1(0, 0)
-        load_x(5)
-        load_w1(0, 1)
-        widen(0, 0, 0, "V")
-        widen(0, 0, 1, "S")
-        widen(0, 1, 0, "V")
+        load_gain()
+        load_x(2, 0, 2)
+        load_w1(1)
+        load_w1(0)
+        widen(0, 0, 0, "S")
+        widen(0, 0, 1, "V")
+        widen(0, 1, 0, "S")
         widen(0, 1, 1, "V")
         widen(1, 0, 0, "S")
         widen(1, 0, 1, "V")
-        widen(1, 1, 0, "V")
-        widen(1, 1, 1, "S")
-        widen(2, 0, 0, "S")
-        widen(2, 0, 1, "S")
-        widen(2, 1, 0, "V")
-        widen(2, 1, 1, "V")
-        widen(3, 0, 0, "V")
-        widen(3, 0, 1, "S")
-        widen(3, 1, 0, "V")
         turn(0, 0)
-        widen(3, 1, 1, "V")
-        widen(4, 0, 0, "V")
-        widen(4, 0, 1, "V")
-        widen(4, 1, 0, "S")
+        widen(1, 1, 0, "V")
+        widen(1, 1, 1, "V")
+        widen(2, 0, 0, "N")
+        widen(2, 0, 1, "N")
+        widen(2, 1, 0, "N")
         gather(0, 0)
-        widen(4, 1, 1, "V")
-        turn(0, 1)
-        load_x(6)
-        group_w1(0, 0, 0, "V")
-        gather(0, 1)
-        turn(1, 0)
-        load_gain()
-        load_w1(1, 1)
-        load_x(7)
-        group_w1(1, 0, 0, "P")
-        gather(1, 0)
-        turn(1, 1)
-        drain_w1(1, 0, 0, "S")
-        group_w1(0, 0, 1, "V")
-        quant_x(0)
-        gather(1, 1)
-        turn(2, 0)
-        group_w1(1, 0, 1, "S")
+        widen(2, 1, 1, "N")
+        widen(3, 0, 0, "S")
         load_w2(0)
         load_w2(2)
         load_w2(4)
@@ -325,10 +296,25 @@ def tile_image_token_merger_d4_kernel(tc, x_bytes, x_scale, w1, gain, w2_words, 
         load_w2(3)
         load_w2(5)
         load_w2(7)
-        gather(2, 0)
-        group_w1(0, 1, 0, "V")
-        turn(2, 1)
-        quant_w1(0, 0, 0)
+        widen(3, 0, 1, "S")
+        widen(3, 1, 0, "N")
+        widen(3, 1, 1, "N")
+        turn(0, 1)
+        widen(4, 0, 0, "V")
+        widen(4, 0, 1, "V")
+        widen(4, 1, 0, "N")
+        widen(4, 1, 1, "N")
+        gather(0, 1)
+        group_w1(1, 0, 0, "V")
+        turn(1, 0)
+        quant_x(0)
+        group_w1(1, 0, 1, "V")
+        load_x(2, 2, 4)
+        gather(1, 0)
+        group_w1(0, 0, 0, "V")
+        turn(1, 1)
+        quant_w1(1, 0, 0)
+        group_w1(0, 0, 1, "V")
         load_w2_scales(0, 0)
         load_w2_scales(0, 1)
         load_w2_scales(0, 2)
@@ -337,31 +323,44 @@ def tile_image_token_merger_d4_kernel(tc, x_bytes, x_scale, w1, gain, w2_words, 
         load_w2_scales(1, 1)
         load_w2_scales(1, 2)
         load_w2_scales(1, 3)
-        quant_w1(1, 0, 0)
-        group_w1(1, 1, 0, "V")
-        gather(2, 1)
-        turn(3, 0)
-        quant_w1(0, 0, 1)
-        group_w1(0, 1, 1, "P")
-        gather(3, 0)
+        gather(1, 1)
+        load_x(3, 0, 4)
         quant_w1(1, 0, 1)
-        turn(3, 1)
-        drain_w1(0, 1, 1, "S")
+        turn(2, 0)
+        group_w1(1, 1, 0, "S")
+        gather(2, 0)
+        group_w1(1, 1, 1, "S")
+        quant_w1(0, 0, 0)
+        turn(2, 1)
+        load_bias()
+        warm_up()
+        warm_up()
+        warm_up()
+        group_w1(0, 1, 0, "S")
+        quant_w1(0, 0, 1)
+        warm_up()
+        gather(2, 1)
+        quant_w1(1, 1, 0)
         quant_x(1)
-        group_w1(1, 1, 1, "V")
+        group_w1(0, 1, 1, "V")
+        turn(3, 0)
+        quant_w1(1, 1, 1)
+        quant_w1(0, 1, 0)
+        gather(3, 0)
+        quant_w1(0, 1, 1)
+        turn(3, 1)
         gather(3, 1)
         turn(4, 0)
-        quant_w1(0, 1, 0)
-        quant_w1(1, 1, 0)
-        load_bias()
-        quant_w1(0, 1, 1)
-        quant_w1(1, 1, 1)
+        turn_gain()
         gather(4, 0)
         turn(4, 1)
-        turn_gain()
-        gather(4, 1)
-        gather_gain()
         quant_x(3)
+        gather(4, 1)
+        warm_up()
+        quant_x(4)
+        quant_x(2)
+        warm_up()
+        gather_gain()
         first_product(0, 0)
         gelu(0, 0)
         first_product(0, 1)
@@ -370,12 +369,10 @@ def tile_image_token_merger_d4_kernel(tc, x_bytes, x_scale, w1, gain, w2_words, 
         gelu(1, 0)
         first_product(1, 1)
         gelu(1, 1)
-        quant_x(2)
         first_product(2, 0)
         gelu(2, 0)
         first_product(2, 1)
         gelu(2, 1)
-        quant_x(4)
         first_product(3, 0)
         gelu(3, 0)
         first_product(3, 1)
@@ -384,167 +381,167 @@ def tile_image_token_merger_d4_kernel(tc, x_bytes, x_scale, w1, gain, w2_words, 
         gelu(4, 0)
         first_product(4, 1)
         gelu(4, 1)
-        apply_gain(0, 0)
         apply_gain(0, 1)
         first_product(5, 0)
         gelu(5, 0)
         first_product(5, 1)
         gelu(5, 1)
-        apply_gain(1, 0)
-        quant_z(0)
+        apply_gain(0, 0)
         apply_gain(1, 1)
-        apply_gain(2, 0)
+        quant_z(0)
+        apply_gain(1, 0)
         first_product(6, 0)
         gelu(6, 0)
         first_product(6, 1)
         gelu(6, 1)
+        apply_gain(2, 1)
         quant_z(1)
         second_product(0, 0)
-        apply_gain(2, 1)
-        second_product(0, 1)
-        apply_gain(3, 0)
-        quant_z(2)
+        apply_gain(2, 0)
+        apply_gain(3, 1)
         first_product(7, 0)
         gelu(7, 0)
         first_product(7, 1)
         gelu(7, 1)
-        second_product(1, 0)
-        widen(5, 0, 0, "V")
+        quant_z(2)
+        widen(5, 0, 0, "S")
+        second_product(0, 1)
         widen(5, 0, 1, "S")
         widen(5, 1, 0, "V")
-        widen(5, 1, 1, "S")
+        widen(5, 1, 1, "V")
         widen(6, 0, 0, "V")
+        second_product(1, 0)
         widen(6, 0, 1, "V")
-        widen(6, 1, 0, "S")
+        widen(6, 1, 0, "V")
         widen(6, 1, 1, "V")
         widen(7, 0, 0, "V")
         widen(7, 0, 1, "V")
+        apply_gain(3, 0)
         widen(7, 1, 0, "V")
         widen(7, 1, 1, "V")
-        apply_gain(3, 1)
-        second_product(1, 1)
-        apply_gain(4, 0)
+        apply_gain(4, 1)
         quant_z(3)
-        second_product(2, 0)
+        second_product(1, 1)
         first_product(8, 0)
         gelu(8, 0)
         first_product(8, 1)
         gelu(8, 1)
-        apply_gain(4, 1)
-        second_product(2, 1)
+        second_product(2, 0)
+        apply_gain(4, 0)
         turn(5, 0)
         turn(5, 1)
         turn(6, 0)
         turn(6, 1)
         turn(7, 0)
         turn(7, 1)
-        apply_gain(5, 0)
         gather(5, 0)
         gather(5, 1)
+        apply_gain(5, 1)
         gather(6, 0)
-        quant_z(4)
         gather(6, 1)
-        second_product(3, 0)
         gather(7, 0)
         gather(7, 1)
-        apply_gain(5, 1)
-        second_product(3, 1)
+        quant_z(4)
+        quant_x(5)
+        second_product(2, 1)
+        second_product(3, 0)
+        apply_gain(5, 0)
+        finish(0, 0)
         first_product(9, 0)
         gelu(9, 0)
         first_product(9, 1)
         gelu(9, 1)
-        apply_gain(6, 0)
-        quant_x(5)
-        finish(0, 0)
-        quant_z(5)
-        second_product(4, 0)
-        finish(0, 1)
         apply_gain(6, 1)
-        apply_gain(7, 0)
+        quant_z(5)
+        second_product(3, 1)
+        second_product(4, 0)
+        apply_gain(6, 0)
+        finish(0, 1)
+        apply_gain(7, 1)
+        quant_x(7)
         first_product(10, 0)
         gelu(10, 0)
         first_product(10, 1)
         gelu(10, 1)
-        quant_z(6)
-        quant_x(6)
         second_product(4, 1)
+        quant_z(6)
         second_product(5, 0)
-        apply_gain(7, 1)
-        apply_gain(8, 0)
+        apply_gain(7, 0)
+        apply_gain(8, 1)
+        second_product(5, 1)
         quant_z(7)
         first_product(11, 0)
         gelu(11, 0)
         first_product(11, 1)
         gelu(11, 1)
-        second_product(5, 1)
+        apply_gain(8, 0)
         second_product(6, 0)
-        apply_gain(8, 1)
-        apply_gain(9, 0)
-        quant_z(8)
+        apply_gain(9, 1)
+        quant_x(6)
         second_product(6, 1)
+        quant_z(8)
+        apply_gain(9, 0)
         second_product(7, 0)
         first_product(12, 0)
         gelu(12, 0)
         first_product(12, 1)
         gelu(12, 1)
-        apply_gain(9, 1)
-        apply_gain(10, 0)
         finish(1, 0)
-        quant_z(9)
-        second_product(7, 1)
-        second_product(8, 0)
-        quant_x(7)
         apply_gain(10, 1)
+        second_product(7, 1)
+        quant_z(9)
+        apply_gain(10, 0)
+        finish(1, 1)
+        second_product(8, 0)
+        apply_gain(11, 1)
         first_product(13, 0)
         gelu(13, 0)
         first_product(13, 1)
         gelu(13, 1)
-        apply_gain(11, 0)
-        finish(1, 1)
         quant_z(10)
+        apply_gain(11, 0)
         second_product(9, 0)
+        apply_gain(12, 1)
         second_product(8, 1)
-        apply_gain(11, 1)
-        apply_gain(12, 0)
+        quant_z(11)
         first_product(14, 0)
         gelu(14, 0)
         first_product(14, 1)
         gelu(14, 1)
-        quant_z(11)
+        apply_gain(12, 0)
         second_product(10, 0)
+        apply_gain(13, 1)
         second_product(9, 1)
-        apply_gain(12, 1)
-        apply_gain(13, 0)
         quant_z(12)
+        apply_gain(13, 0)
         second_product(11, 0)
         first_product(15, 0)
         gelu(15, 0)
         first_product(15, 1)
         gelu(15, 1)
-        second_product(10, 1)
-        apply_gain(13, 1)
-        apply_gain(14, 0)
-        finish(2, 0)
-        quant_z(13)
-        second_product(12, 0)
-        second_product(11, 1)
         apply_gain(14, 1)
-        apply_gain(15, 0)
-        second_product(13, 0)
+        finish(2, 0)
+        second_product(10, 1)
+        quant_z(13)
+        apply_gain(14, 0)
+        second_product(12, 0)
+        apply_gain(15, 1)
+        second_product(11, 1)
         quant_z(14)
         finish(2, 1)
-        apply_gain(15, 1)
+        apply_gain(15, 0)
+        second_product(13, 0)
         second_product(14, 0)
-        quant_z_last(15, 1)
         quant_z_last(15, 0)
         second_product(12, 1)
         second_product(13, 1)
         second_product(14, 1)
+        second_last(15, 0, 0)
+        quant_z_last(15, 1)
+        second_last(15, 1, 0)
+        finish_last(3, 0, 0)
+        finish_last(3, 0, 1)
         second_last(15, 0, 1)
         second_last(15, 1, 1)
         finish_last(3, 1, 0)
         finish_last(3, 1, 1)
-        second_last(15, 0, 0)
-        second_last(15, 1, 0)
-        finish_last(3, 0, 0)
-        finish_last(3, 0, 1)

from contextlib import ExitStack

import concourse.mybir as mybir
from concourse.masks import make_identity

T, R, K, F, N = 2048, 4, 1024, 1024, 1024
FLOPS = 2 * T * K * F + 2 * (T // R) * (R * F) * N

F32 = mybir.dt.float32
BF16 = mybir.dt.bfloat16
I32 = mybir.dt.int32
U32 = mybir.dt.uint32
U8 = mybir.dt.uint8
FP8 = mybir.dt.float8_e4m3fn
FP8X4 = mybir.dt.float8_e4m3fn_x4
FP4X4 = mybir.dt.float4_e2m1fn_x4
MULT = mybir.AluOpType.mult
ADD = mybir.AluOpType.add
COPY = mybir.ActivationFunctionType.Copy
GELU = mybir.ActivationFunctionType.Gelu_apprx_tanh

P = 128
GROUPS = 4
PAIRS = 8
XW_BUFS = 24
UNITS = [(0, 0), (1, 0), (0, 1), (1, 1)] + [(pair, g) for pair in range(2, PAIRS) for g in range(2)]


def tile_image_token_merger_d4_kernel(tc, x_bytes, x_scale, w1, gain, w2_words, w2_scales, b, out):
    nc = tc.nc
    with ExitStack() as ctx:
        keep = ctx.enter_context(tc.tile_pool(name="keep", bufs=1))
        work = ctx.enter_context(tc.tile_pool(name="work", bufs=4))
        psum = ctx.enter_context(tc.psum_pool(name="psum", bufs=1))
        ctx.enter_context(tc.manual_schedule())

        ident = keep.tile([P, P], F32, name="ident")
        make_identity(nc, ident[:])
        warm = keep.tile([P, 8], F32, name="warm")
        nc.vector.memset(warm[:, 0:1], 0.0)
        nc.scalar.activation(out=warm[:, 4:5], in_=warm[:, 0:1], func=GELU)

        gain_rows = keep.tile([P, 512], BF16, name="gain_rows")
        nc.vector.memset(gain_rows[:].bitcast(I32), 0)
        w2s = [keep.tile([P, R, N], U8, name="w2s%d" % g, align_bytes=64) for g in range(2)]
        for g in range(2):
            nc.vector.memset(w2s[g][:].rearrange("p j n -> p (j n)").bitcast(I32), 0)

        xs = [keep.tile([P, 1, 32], F32, name="xs0"), keep.tile([P, GROUPS - 1, 32], F32, name="xs1")]
        xb = [keep.tile([P, R * K], U8, name="xb%d" % i) for i in range(GROUPS)]
        w1raw = [keep.tile([P, 4, F], BF16, name="w1raw%d" % c) for c in range(2)]
        w2w = [keep.tile([P, 2 * N], U8, name="w2w%d" % i, align_bytes=64) for i in range(8)]
        bias = keep.tile([P, N], BF16, name="bias")
        x_rows = x_bytes.rearrange("(G m j) k -> G m (j k)", m=P, j=R)
        w1_rows = w1.rearrange("(c p s) f -> c p s f", p=P, s=4)
        w2s_rows = w2_scales.rearrange("(j g) r n -> g r j n", g=2)

        def load_x(grp, lo, hi):
            cols = slice(K * lo, K * hi)
            nc.sync.dma_start(out=xb[grp][:, cols], in_=x_rows[grp][:, cols])

        def load_w1(c):
            nc.sync.dma_start(out=w1raw[c][:], in_=w1_rows[c])

        def warm_up():
            if not scratch:
                scratch.append(psum.tile([P, 512], F32, name="scratch", tag="yb", bufs=2))
            nc.tensor.matmul(out=scratch[0][:], lhsT=gain_rows[:, 0:P], rhs=gain_rows[:], start=True, stop=True)

        def load_w2_scales(g, q):
            nc.sync.dma_start(
                out=w2s[g][32 * q : 32 * q + 4, :, :].bitcast(I32),
                in_=w2s_rows[g, 4 * q : 4 * q + 4].bitcast(I32),
            )

        def load_w2(i):
            nc.sync.dma_start(out=w2w[i][:].bitcast(I32), in_=w2_words[i].bitcast(I32))

        modes, scratch = {}, []
        xw, xt, xg, xq, w1g, w1q, hb, act, zg, zq, yb = {}, {}, {}, {}, {}, {}, {}, {}, {}, {}, {}

        def widen(pair, jj, c, mode):
            xw[pair, jj, c] = work.tile([P, 512], BF16, name="xw", bufs=XW_BUFS)
            modes[pair, jj, c] = mode
            dst = xw[pair, jj, c]
            if mode == "D":
                dst = work.tile([P, 512], BF16, name="xnat", bufs=2)
            for q in range(4):
                blk = 4 * c + q
                col = 8 * (2 * (pair % 2) + jj) + blk
                src = xb[pair // 2][:, 128 * col : 128 * (col + 1)].bitcast(FP8)
                scale = xs[0][:, 0, col : col + 1] if pair < 2 else xs[1][:, pair // 2 - 1, col : col + 1]
                if mode == "V":
                    nc.vector.tensor_scalar(
                        out=dst[:].rearrange("m (u p e) -> m p u e", u=2, e=2)[:, 32 * q : 32 * (q + 1), :, :],
                        in0=src.rearrange("m (p u e) -> m p u e", u=2, e=2),
                        scalar1=scale,
                        scalar2=None,
                        op0=MULT,
                    )
                elif mode == "N":
                    nc.vector.tensor_scalar(
                        out=dst[:, 128 * q : 128 * (q + 1)], in0=src, scalar1=scale, scalar2=None, op0=MULT
                    )
                else:
                    nc.scalar.activation(out=dst[:, 128 * q : 128 * (q + 1)], in_=src, func=COPY, scale=scale)
            if mode == "D":
                nc.scalar.copy(
                    out=xw[pair, jj, c][:].bitcast(F32).rearrange("m (u p) -> m u p", u=2),
                    in_=dst[:].bitcast(F32).rearrange("m (p u) -> m u p", u=2),
                )

        def turn(pair, jj):
            xt[pair, jj] = psum.tile([P, 2, 2, P], F32, name="xt", tag="ring", bufs=6)
            for c in range(2):
                words = xw[pair, jj, c][:].bitcast(F32)
                for u in range(2):
                    src = words[:, u : 256 : 2] if modes[pair, jj, c] in ("S", "N") else words[:, P * u : P * (u + 1)]
                    nc.tensor.transpose(xt[pair, jj][:, c, u, :], src, ident[:])

        def gather(pair, jj):
            if pair not in xg:
                xg[pair] = work.tile([P, 2, 2, P, 2], F32, name="xg", bufs=5, align_bytes=64)
            nc.scalar.copy(out=xg[pair][:, :, jj, :, :], in_=xt[pair, jj][:].rearrange("p c u m -> p c m u"))

        def quant_x(pair):
            codes = work.tile([P, 512], U32, name="xcodes", bufs=6, align_bytes=64)
            scales = work.tile([P, 512], U8, name="xscales", bufs=6, align_bytes=64)
            src = xg[pair][:].rearrange("p c jj m u -> p (c jj m u)").bitcast(BF16)
            nc.vector.quantize_mx(out=codes[:].bitcast(FP8X4), scales=scales[:], in_=src)
            xq[pair] = (codes, scales)

        def group_w1(c, g, mh, mode):
            if (c, g) not in w1g:
                w1g[c, g] = keep.tile([P, 4, P, 4], BF16, name="w1g%d%d" % (c, g), align_bytes=64)
            copy = nc.vector.tensor_copy if mode == "V" else nc.scalar.copy
            part = slice(32 * mh, 32 * (mh + 1))
            copy(
                out=w1g[c, g][:].rearrange("p t (a m) s -> p a t m s", m=2)[:, part],
                in_=w1raw[c][:, :, 512 * g : 512 * (g + 1)].rearrange("p s (a m t) -> p a t m s", m=2, t=4)[:, part],
            )

        def quant_w1(c, g, u):
            codes = keep.tile([P, 256], U32, name="w1codes%d%d%d" % (c, g, u), align_bytes=64)
            scales = keep.tile([P, 256], U8, name="w1scales%d%d%d" % (c, g, u), align_bytes=64)
            src = w1g[c, g][:, 2 * u : 2 * u + 2].rearrange("p t m s -> p (t m s)")
            nc.vector.quantize_mx(out=codes[:].bitcast(FP8X4), scales=scales[:], in_=src)
            w1q[c, g, u] = (codes, scales)

        def first_product(s, u):
            pair, g = UNITS[s]
            hb[s, u] = psum.tile([P, 2, 256], F32, name="hb", tag="ring", bufs=6)
            for e in range(2):
                cols = slice(P * e, P * (e + 1))
                for c in range(2):
                    toks = slice(256 * c, 256 * (c + 1))
                    nc.tensor.matmul_mx(
                        out=hb[s, u][:, e, :],
                        lhsT=w1q[c, g, u][0][:, cols].bitcast(FP8X4),
                        lhsT_scale=w1q[c, g, u][1][:, cols],
                        rhs=xq[pair][0][:, toks].bitcast(FP8X4),
                        rhs_scale=xq[pair][1][:, toks],
                        start=(c == 0),
                        stop=(c == 1),
                    )

        def gelu(s, u):
            if s not in act:
                act[s] = work.tile([P, 2, 256, 2], F32, name="act", bufs=7)
            nc.scalar.activation(out=act[s][:, u, :, :], in_=hb[s, u][:].rearrange("p e n -> p n e"), func=GELU)

        def apply_gain(s, jj):
            pair, g = UNITS[s]
            if s not in zg:
                zg[s] = work.tile([P, 2, P, 2, 2], BF16, name="zg", bufs=3, align_bytes=64)
            row = 2 * (2 * (pair % 2) + jj) + g
            nc.vector.tensor_tensor(
                out=zg[s][:, jj, :, :, :],
                in0=act[s][:, :, P * jj : P * (jj + 1), :].rearrange("p u m e -> p m u e"),
                in1=gain_sb[0][:, row : row + 1, :, :].to_broadcast([P, P, 2, 2]),
                op=MULT,
            )

        def quant_z(s):
            codes = work.tile([P, 256], U32, name="zcodes", bufs=6, align_bytes=64)
            scales = work.tile([P, 256], U8, name="zscales", bufs=6, align_bytes=64)
            src = zg[s][:].rearrange("p jj m u e -> p (jj m u e)")
            nc.vector.quantize_mx(out=codes[:].bitcast(FP8X4), scales=scales[:], in_=src)
            zq[s] = (codes, scales)

        def quant_z_last(s, jj):
            codes = work.tile([P, P], U32, name="lcodes", bufs=2, align_bytes=64)
            scales = work.tile([P, P], U8, name="lscales", bufs=2, align_bytes=64)
            src = zg[s][:, jj].rearrange("p m u e -> p (m u e)")
            nc.vector.quantize_mx(out=codes[:].bitcast(FP8X4), scales=scales[:], in_=src)
            zq[s, jj] = (codes, scales)

        def second_last(s, jj, half):
            pair, g = UNITS[s]
            j = 2 * (pair % 2) + jj
            nc.tensor.matmul_mx(
                out=yb[s // 4, half][:],
                lhsT=zq[s, jj][0][:].bitcast(FP8X4),
                lhsT_scale=zq[s, jj][1][:],
                rhs=w2w[2 * j + g][:, N * half : N * (half + 1)].bitcast(FP4X4),
                rhs_scale=w2s[g][:, j, 512 * half : 512 * (half + 1)],
                start=False,
                stop=(jj == 1),
            )

        def finish_last(grp, half, q):
            cols = slice(512 * half + 256 * q, 512 * half + 256 * (q + 1))
            y = work.tile([P, 256], F32, name="ylast", bufs=4)
            nc.vector.tensor_tensor(out=y[:], in0=yb[grp, half][:, 256 * q : 256 * (q + 1)], in1=bias[:, cols], op=ADD)
            nc.sync.dma_start(out=out[P * grp : P * (grp + 1), cols], in_=y[:])

        def second_product(s, half):
            pair, g = UNITS[s]
            if True:
                if s % 4 == 0:
                    yb[s // 4, half] = psum.tile([P, 512], F32, name="yb", bufs=2)
                for jj in range(2):
                    j = 2 * (pair % 2) + jj
                    rows = slice(P * jj, P * (jj + 1))
                    nc.tensor.matmul_mx(
                        out=yb[s // 4, half][:],
                        lhsT=zq[s][0][:, rows].bitcast(FP8X4),
                        lhsT_scale=zq[s][1][:, rows],
                        rhs=w2w[2 * j + g][:, N * half : N * (half + 1)].bitcast(FP4X4),
                        rhs_scale=w2s[g][:, j, 512 * half : 512 * (half + 1)],
                        start=(s % 4 == 0 and jj == 0),
                        stop=(s % 4 == 3 and jj == 1),
                    )

        def finish(grp, half):
            cols = slice(512 * half, 512 * (half + 1))
            y = work.tile([P, 512], F32, name="y", bufs=3)
            nc.vector.tensor_tensor(out=y[:], in0=yb[grp, half][:], in1=bias[:, cols], op=ADD)
            nc.sync.dma_start(out=out[P * grp : P * (grp + 1), cols], in_=y[:])

        gain_t, gain_sb = [], []

        def turn_gain():
            gain_t.append(psum.tile([P, 2, P], F32, name="gain_t", tag="yb", bufs=2))
            gain_words = gain_rows[:].bitcast(F32)
            for u in range(2):
                nc.tensor.transpose(gain_t[0][:, u, :], gain_words[:, u : 256 : 2], ident[:])

        def gather_gain():
            gain_sb.append(keep.tile([P, 8, 2, 2], BF16, name="gain_sb"))
            nc.scalar.copy(
                out=gain_sb[0][:].rearrange("p r u e -> p r (u e)").bitcast(F32),
                in_=gain_t[0][:, :, 0:8].rearrange("p u r -> p r u"),
            )

        def load_xs(i):
            rows = x_scale.rearrange("(G m j) c -> m G (j c)", m=P, j=R)
            nc.sync.dma_start(out=xs[i][:], in_=rows[:, 0:1, :] if i == 0 else rows[:, 1:GROUPS, :])

        def load_gain():
            nc.sync.dma_start(out=gain_rows[0:8, :], in_=gain.rearrange("(r f) -> r f", f=512))

        def load_bias():
            nc.sync.dma_start(out=bias[:], in_=b.partition_broadcast(P))

        load_x(0, 0, 1)
        load_xs(0)
        load_x(0, 1, 2)
        load_x(0, 2, 4)
        load_x(1, 0, 4)
        load_xs(1)
        load_gain()
        load_x(2, 0, 2)
        load_w1(1)
        load_w1(0)
        widen(0, 0, 0, "S")
        widen(0, 0, 1, "V")
        widen(0, 1, 0, "S")
        widen(0, 1, 1, "V")
        widen(1, 0, 0, "S")
        widen(1, 0, 1, "V")
        turn(0, 0)
        widen(1, 1, 0, "V")
        widen(1, 1, 1, "V")
        widen(2, 0, 0, "N")
        widen(2, 0, 1, "N")
        widen(2, 1, 0, "N")
        gather(0, 0)
        widen(2, 1, 1, "N")
        widen(3, 0, 0, "S")
        load_w2(0)
        load_w2(2)
        load_w2(4)
        load_w2(6)
        load_w2(1)
        load_w2(3)
        load_w2(5)
        load_w2(7)
        widen(3, 0, 1, "S")
        widen(3, 1, 0, "N")
        widen(3, 1, 1, "N")
        turn(0, 1)
        widen(4, 0, 0, "V")
        widen(4, 0, 1, "V")
        widen(4, 1, 0, "N")
        widen(4, 1, 1, "N")
        gather(0, 1)
        group_w1(1, 0, 0, "V")
        turn(1, 0)
        quant_x(0)
        group_w1(1, 0, 1, "V")
        load_x(2, 2, 4)
        gather(1, 0)
        group_w1(0, 0, 0, "V")
        turn(1, 1)
        quant_w1(1, 0, 0)
        group_w1(0, 0, 1, "V")
        load_w2_scales(0, 0)
        load_w2_scales(0, 1)
        load_w2_scales(0, 2)
        load_w2_scales(0, 3)
        load_w2_scales(1, 0)
        load_w2_scales(1, 1)
        load_w2_scales(1, 2)
        load_w2_scales(1, 3)
        gather(1, 1)
        load_x(3, 0, 4)
        quant_w1(1, 0, 1)
        turn(2, 0)
        group_w1(1, 1, 0, "S")
        gather(2, 0)
        group_w1(1, 1, 1, "S")
        quant_w1(0, 0, 0)
        turn(2, 1)
        load_bias()
        warm_up()
        warm_up()
        warm_up()
        group_w1(0, 1, 0, "S")
        quant_w1(0, 0, 1)
        warm_up()
        gather(2, 1)
        quant_w1(1, 1, 0)
        quant_x(1)
        group_w1(0, 1, 1, "V")
        turn(3, 0)
        quant_w1(1, 1, 1)
        quant_w1(0, 1, 0)
        gather(3, 0)
        quant_w1(0, 1, 1)
        turn(3, 1)
        gather(3, 1)
        turn(4, 0)
        turn_gain()
        gather(4, 0)
        turn(4, 1)
        quant_x(3)
        gather(4, 1)
        warm_up()
        quant_x(4)
        quant_x(2)
        warm_up()
        gather_gain()
        first_product(0, 0)
        gelu(0, 0)
        first_product(0, 1)
        gelu(0, 1)
        first_product(1, 0)
        gelu(1, 0)
        first_product(1, 1)
        gelu(1, 1)
        first_product(2, 0)
        gelu(2, 0)
        first_product(2, 1)
        gelu(2, 1)
        first_product(3, 0)
        gelu(3, 0)
        first_product(3, 1)
        gelu(3, 1)
        first_product(4, 0)
        gelu(4, 0)
        first_product(4, 1)
        gelu(4, 1)
        apply_gain(0, 1)
        first_product(5, 0)
        gelu(5, 0)
        first_product(5, 1)
        gelu(5, 1)
        apply_gain(0, 0)
        apply_gain(1, 1)
        quant_z(0)
        apply_gain(1, 0)
        first_product(6, 0)
        gelu(6, 0)
        first_product(6, 1)
        gelu(6, 1)
        apply_gain(2, 1)
        quant_z(1)
        second_product(0, 0)
        apply_gain(2, 0)
        apply_gain(3, 1)
        first_product(7, 0)
        gelu(7, 0)
        first_product(7, 1)
        gelu(7, 1)
        quant_z(2)
        widen(5, 0, 0, "S")
        second_product(0, 1)
        widen(5, 0, 1, "S")
        widen(5, 1, 0, "V")
        widen(5, 1, 1, "V")
        widen(6, 0, 0, "V")
        second_product(1, 0)
        widen(6, 0, 1, "V")
        widen(6, 1, 0, "V")
        widen(6, 1, 1, "V")
        widen(7, 0, 0, "V")
        widen(7, 0, 1, "V")
        apply_gain(3, 0)
        widen(7, 1, 0, "V")
        widen(7, 1, 1, "V")
        apply_gain(4, 1)
        quant_z(3)
        second_product(1, 1)
        first_product(8, 0)
        gelu(8, 0)
        first_product(8, 1)
        gelu(8, 1)
        second_product(2, 0)
        apply_gain(4, 0)
        turn(5, 0)
        turn(5, 1)
        turn(6, 0)
        turn(6, 1)
        turn(7, 0)
        turn(7, 1)
        gather(5, 0)
        gather(5, 1)
        apply_gain(5, 1)
        gather(6, 0)
        gather(6, 1)
        gather(7, 0)
        gather(7, 1)
        quant_z(4)
        quant_x(5)
        second_product(2, 1)
        second_product(3, 0)
        apply_gain(5, 0)
        finish(0, 0)
        first_product(9, 0)
        gelu(9, 0)
        first_product(9, 1)
        gelu(9, 1)
        apply_gain(6, 1)
        quant_z(5)
        second_product(3, 1)
        second_product(4, 0)
        apply_gain(6, 0)
        finish(0, 1)
        apply_gain(7, 1)
        quant_x(7)
        first_product(10, 0)
        gelu(10, 0)
        first_product(10, 1)
        gelu(10, 1)
        second_product(4, 1)
        quant_z(6)
        second_product(5, 0)
        apply_gain(7, 0)
        apply_gain(8, 1)
        second_product(5, 1)
        quant_z(7)
        first_product(11, 0)
        gelu(11, 0)
        first_product(11, 1)
        gelu(11, 1)
        apply_gain(8, 0)
        second_product(6, 0)
        apply_gain(9, 1)
        quant_x(6)
        second_product(6, 1)
        quant_z(8)
        apply_gain(9, 0)
        second_product(7, 0)
        first_product(12, 0)
        gelu(12, 0)
        first_product(12, 1)
        gelu(12, 1)
        finish(1, 0)
        apply_gain(10, 1)
        second_product(7, 1)
        quant_z(9)
        apply_gain(10, 0)
        finish(1, 1)
        second_product(8, 0)
        apply_gain(11, 1)
        first_product(13, 0)
        gelu(13, 0)
        first_product(13, 1)
        gelu(13, 1)
        quant_z(10)
        apply_gain(11, 0)
        second_product(9, 0)
        apply_gain(12, 1)
        second_product(8, 1)
        quant_z(11)
        first_product(14, 0)
        gelu(14, 0)
        first_product(14, 1)
        gelu(14, 1)
        apply_gain(12, 0)
        second_product(10, 0)
        apply_gain(13, 1)
        second_product(9, 1)
        quant_z(12)
        apply_gain(13, 0)
        second_product(11, 0)
        first_product(15, 0)
        gelu(15, 0)
        first_product(15, 1)
        gelu(15, 1)
        apply_gain(14, 1)
        finish(2, 0)
        second_product(10, 1)
        quant_z(13)
        apply_gain(14, 0)
        second_product(12, 0)
        apply_gain(15, 1)
        second_product(11, 1)
        quant_z(14)
        finish(2, 1)
        apply_gain(15, 0)
        second_product(13, 0)
        second_product(14, 0)
        quant_z_last(15, 0)
        second_product(12, 1)
        second_product(13, 1)
        second_product(14, 1)
        second_last(15, 0, 0)
        quant_z_last(15, 1)
        second_last(15, 1, 0)
        finish_last(3, 0, 0)
        finish_last(3, 0, 1)
        second_last(15, 0, 1)
        second_last(15, 1, 1)
        finish_last(3, 1, 0)
        finish_last(3, 1, 1)
